import numpy as np
import ml_dtypes


def mxq(x, axis, fmt="e4m3"):
    dtype, down = {"e4m3": (ml_dtypes.float8_e4m3fn, 7), "e5m2": (ml_dtypes.float8_e5m2, 14)}[fmt]
    v = np.moveaxis(np.asarray(x, np.float32).astype(ml_dtypes.bfloat16).astype(np.float64), axis, -1)
    blocks = v.reshape(v.shape[:-1] + (-1, 32))
    amax = np.abs(blocks).max(-1, keepdims=True)
    byte = np.maximum(np.where(amax > 0, np.frexp(amax)[1] - 1 + 127, 0) - down, 1)
    scale = np.exp2(byte - 127.0)
    codes = (blocks / scale).astype(np.float32).astype(dtype).astype(np.float64)
    return np.moveaxis((codes * scale).reshape(v.shape), -1, axis)


WIDE = False


def mx_kscale(k):
    if not WIDE:
        return np.ones(k)
    levels = np.array([10, -10, 5, -5, 0])
    if k % 512:
        return np.exp2(np.random.permutation(np.resize(levels, k // 32))).repeat(32)
    a = np.empty((k // 512, 16))
    for p in range(k // 512):
        a[p, :8] = np.random.permutation(np.resize(levels, 8))
        for g in range(8):
            far = levels[np.abs(levels - a[p, g]) >= 10]
            a[p, g + 8] = far[np.random.randint(len(far))]
    return np.exp2(a.ravel()).repeat(32)


def f64(x):
    return np.asarray(x).astype(np.float64)


def striped(idx):
    return np.tile(idx.reshape(-1, 16).T, (8, 1)).astype(np.uint16)


def unstriped(offs):
    return offs[:16].T.reshape(-1).astype(np.int64)


def striped8(idx):
    return np.concatenate([x.reshape(-1, 16).T for x in idx]).astype(np.uint16)


def runs(offs, k):
    lists = np.stack([offs[16 * r : 16 * r + 16].T.reshape(-1) for r in range(8)]).astype(np.int64)
    return lists[np.arange(k) % 512 // 64]


def pack_weight(w):
    k, n = w.shape
    w = f64(np.asarray(w, np.float32).astype(ml_dtypes.bfloat16)).reshape(k // 32, 32, n)
    amax = np.abs(w).max(1)
    byte = np.clip(np.where(amax > 0, np.frexp(amax)[1] - 1 + 127 - 7, 1), 1, 254)
    scaled = (w * np.exp2(127.0 - byte)[:, None, :]).reshape(k, n).astype(np.float32)
    words = np.ascontiguousarray(scaled.reshape(k // 512, 128, 4, n).transpose(0, 1, 3, 2)).astype(ml_dtypes.float8_e4m3fn).view(np.uint8)
    return words, np.ascontiguousarray(byte.astype(np.uint8).reshape(k // 512, 16, n))


def unpack_weight(words, scales):
    g, p, n, _ = words.shape
    vals = np.ascontiguousarray(words).view(ml_dtypes.float8_e4m3fn).astype(np.float64) * np.repeat(np.exp2(scales.astype(np.float64) - 127.0), 8, axis=1)[..., None]
    return vals.transpose(0, 1, 3, 2).reshape(g * 512, n)


K, T, S, H, G, U = 512, 1024, 512, 512, 2048, 1024


def setup_inputs():
    n = np.random.standard_normal
    s = mx_kscale(K)[:, None]
    packed_xT = pack_weight(n((K, T)) * s)
    packed_dT = pack_weight(n((K, G)) / s)
    return {
        "x_words": packed_xT[0],
        "x_scales": packed_xT[1],
        "w1": (n((K, H)) / np.sqrt(K) / s).astype(np.float32),
        "w2": (n((K, H)) / np.sqrt(K) / s).astype(np.float32),
        "gs": (np.random.uniform(0.5, 1.5, (K, 1)) * s).astype(np.float32),
        "d_words": packed_dT[0],
        "d_scales": packed_dT[1],
        "mem": n((H, U)).astype(np.float32),
        "offs": striped(np.random.permutation(T)[:S]),
        "two": striped(np.random.permutation(T)[:S]),
        "n1": striped8(np.stack([np.random.permutation(S) for _ in range(8)])),
        "n2": striped8(np.stack([np.random.permutation(S) for _ in range(8)])),
        "k1": striped8(np.random.randint(0, G, (8, H))),
        "n3": striped8(np.stack([np.random.permutation(U)[:S] for _ in range(8)])),
    }


def reference(x_words, x_scales, w1, w2, gs, d_words, d_scales, mem, offs, two, n1, n2, k1, n3):
    d_k1 = unpack_weight(d_words, d_scales)[np.arange(K)[:, None], runs(k1, K)]
    xq = unpack_weight(x_words, x_scales)[:, unstriped(offs)]
    y = mxq(f64(w1), 0, "e4m3").T @ xq
    x_two = unpack_weight(x_words, x_scales)[:, unstriped(two)]
    d = mxq(f64(w2), 0, "e4m3").T @ x_two
    z = f64(gs) * (y * (np.tanh(d[np.arange(H)[:, None], runs(n1, H)] - (d[np.arange(H)[:, None], runs(n2, H)]))))
    h = 0.0625 * ((d_k1.T @ mxq(z, 0, "e4m3")))
    nw = np.maximum(h, 0.5 * (f64(mem)[np.arange(H)[:, None], runs(n3, H)]))
    out = f64(mem).copy()
    out[np.arange(H)[:, None], runs(n3, H)] = nw
    return out

@@ -1,0 +1,224 @@
+from contextlib import ExitStack
+
+import concourse.mybir as mybir
+
+K, T, S, H, G, U = 512, 1024, 512, 512, 2048, 1024
+FLOPS = 3 * 2 * 512 * 512 * 512
+
+F32 = mybir.dt.float32
+BF16 = mybir.dt.bfloat16
+I32 = mybir.dt.int32
+U32 = mybir.dt.uint32
+U16 = mybir.dt.uint16
+U8 = mybir.dt.uint8
+FP8X4 = mybir.dt.float8_e4m3fn_x4
+ALU = mybir.AluOpType
+ACT = mybir.ActivationFunctionType
+
+P = 128
+PACK = 4
+
+
+def tile_picked_twqjointbpagex_none_p_kernel(
+    tc, x_words, x_scales, w1, w2, gs, d_words, d_scales, mem, offs, two, n1, n2, k1, n3, out
+):
+    nc = tc.nc
+    with ExitStack() as ctx:
+        sb = ctx.enter_context(tc.tile_pool(name="sb", bufs=1))
+        psum = ctx.enter_context(tc.psum_pool(name="psum", bufs=1))
+
+        def load_list(src, name):
+            tile = sb.tile([P, S // 16], U16, name=name)
+            nc.sync.dma_start(tile[:], src)
+            return tile
+
+        def load_words(src, width, name):
+            tile = sb.tile([P, width], U32, name=name)
+            nc.sync.dma_start(tile[:].bitcast(I32), src[0].rearrange("p c r -> p (c r)").bitcast(I32))
+            return tile
+
+        def load_scales(src, width, first, queue, name):
+            tile = sb.tile([P, width], U8, name=name)
+            nc.gpsimd.memset(tile[:].bitcast(I32), 0)
+            for q in range(4):
+                queue.dma_start(
+                    tile[32 * q + first : 32 * q + first + 4, :].bitcast(I32),
+                    src[0, 4 * q : 4 * q + 4, :].bitcast(I32),
+                )
+            return tile
+
+        def load_weight_half(w, half, name):
+            raw = sb.tile([P, PACK, H // 2], F32, name=name)
+            cols = slice(half * (H // 2), (half + 1) * (H // 2))
+            nc.sync.dma_start(raw[:], w.rearrange("(p j) c -> p j c", j=PACK)[:, :, cols])
+            return raw
+
+        def deal_weight(halves, name):
+            grouped = sb.tile([P, PACK, P, PACK], BF16, name=name, align_bytes=64)
+            for half, raw in enumerate(halves):
+                nc.scalar.copy(
+                    grouped[:, :, half * 64 : (half + 1) * 64, :].rearrange("p t m j -> p m j t"),
+                    raw[:].rearrange("p j (m t) -> p m j t", t=PACK),
+                )
+            return grouped
+
+        def quantize(grouped, name):
+            codes = sb.tile([P, 512], U32, name=name + "_codes", align_bytes=64)
+            scales = sb.tile([P, 512], U8, name=name + "_scales", align_bytes=64)
+            nc.vector.quantize_mx(out=codes[:].bitcast(FP8X4), scales=scales[:], in_=grouped)
+            return codes, scales
+
+        def gather(window, lst, dtype, name):
+            picked = sb.tile([P, 512], dtype, name=name, align_bytes=64)
+            nc.vector.tensor_copy(picked[:], window[:].indirect(lst[:]))
+            return picked
+
+        def product(lhs, rhs, t, tag):
+            acc = psum.tile([P, S], F32, name="acc_%s%d" % (tag, t), tag="%s%d" % (tag, t))
+            cols = slice(t * P, (t + 1) * P)
+            nc.tensor.matmul_mx(
+                out=acc[:],
+                lhsT=lhs[0][:, cols].bitcast(FP8X4),
+                lhsT_scale=lhs[1][:, cols],
+                rhs=rhs[0][:].bitcast(FP8X4),
+                rhs_scale=rhs[1][:],
+                start=True,
+                stop=True,
+            )
+            return acc
+
+        two_l = load_list(two, "two_l")
+        offs_l = load_list(offs, "offs_l")
+        xs = load_scales(x_scales, T, 0, nc.scalar, "xs")
+        xw = load_words(x_words, T, "xw")
+        w2_raw = [load_weight_half(w2, h, "w2_raw%d" % h) for h in range(2)]
+        dw = load_words(d_words, G, "dw")
+        k1_l = load_list(k1, "k1_l")
+        ds = load_scales(d_scales, G, 14, nc.sync, "ds")
+        n2_l = load_list(n2, "n2_l")
+        n1_l = load_list(n1, "n1_l")
+        w1_raw = [load_weight_half(w1, h, "w1_raw%d" % h) for h in range(2)]
+        gs_t = sb.tile([P, PACK], F32, name="gs_t")
+        nc.sync.dma_start(gs_t[:], gs.rearrange("(p t) o -> p (t o)", t=PACK))
+        n3_l = load_list(n3, "n3_l")
+        pages = []
+        for t in range(PACK):
+            page = sb.tile([P, U], F32, name="page%d" % t)
+            nc.sync.dma_start(page[:], mem.rearrange("(p t) u -> p t u", t=PACK)[:, t, :])
+            pages.append(page)
+
+        zero = sb.tile([P, 1], F32, name="zero")
+        nc.gpsimd.memset(zero[:], 0.0)
+        bias0 = sb.tile([P, 1], F32, name="bias0")
+        nc.scalar.activation(bias0[:], zero[:], ACT.Tanh)
+
+        d_win = []
+        for t in range(PACK):
+            win = sb.tile([P, 2 * S], F32, name="d_win%d" % t)
+            nc.vector.memset(win[:, S:], 0.0)
+            d_win.append(win)
+        dk_scales = sb.tile([P, H], U8, name="dk_scales", align_bytes=64)
+        nc.gpsimd.memset(dk_scales[:].bitcast(I32), 0)
+
+        x2_s = gather(xs, two_l, U8, "x2_s")
+        x1_s = gather(xs, offs_l, U8, "x1_s")
+        x2_w = gather(xw, two_l, U32, "x2_w")
+        x1_w = gather(xw, offs_l, U32, "x1_w")
+
+        w2_g = deal_weight(w2_raw, "w2_g")
+        w2_q = quantize(w2_g[:].rearrange("p t m j -> p (t m j)"), "w2")
+        for t in range(PACK):
+            acc = product(w2_q, (x2_w, x2_s), t, "a")
+            nc.scalar.copy(d_win[t][:, :S], acc[:])
+
+        dk_w_raw = gather(dw, k1_l, U32, "dk_w_raw")
+        dk_s_raw = gather(ds, k1_l, U8, "dk_s_raw")
+        dk_words = sb.tile([P, H], U32, name="dk_words", align_bytes=64)
+        nc.vector.tensor_copy(
+            dk_words[:].rearrange("p (t a b) -> p a t b", t=PACK, b=4),
+            dk_w_raw[:].rearrange("p (a b t) -> p a t b", t=PACK, b=4),
+        )
+        dk_s_dealt = sb.tile([P, H], U8, name="dk_s_dealt", align_bytes=64)
+        nc.vector.tensor_copy(
+            dk_s_dealt[:].rearrange("p (t a b) -> p a t b", t=PACK, b=16),
+            dk_s_raw[:].rearrange("p (a b t) -> p a t b", t=PACK, b=16),
+        )
+        nc.sync.dma_start(dk_scales[0:100, :].bitcast(I32), dk_s_dealt[14:114, :].bitcast(I32))
+
+        w1_g = deal_weight(w1_raw, "w1_g")
+        w1_q = quantize(w1_g[:].rearrange("p t m j -> p (t m j)"), "w1")
+        y_acc = [product(w1_q, (x1_w, x1_s), t, "b") for t in range(PACK)]
+
+        z = sb.tile([P, PACK, S], F32, name="z")
+        second = [None] * PACK
+        th = [None] * PACK
+
+        def take_second(t):
+            second[t] = sb.tile([P, S], F32, name="second%d" % t, tag="st%d" % t)
+            nc.vector.tensor_copy(second[t][:], d_win[t][:].indirect(n2_l[:]))
+
+        def difference(t):
+            diff = sb.tile([P, S], F32, name="diff%d" % t)
+            nc.vector.tensor_tensor(diff[:], d_win[t][:].indirect(n1_l[:]), second[t][:], ALU.subtract)
+            th[t] = sb.tile([P, S], F32, name="th%d" % t)
+            nc.scalar.activation(th[t][:], diff[:], ACT.Tanh, bias=bias0[:])
+
+        def weigh(t):
+            nc.vector.scalar_tensor_tensor(
+                z[:, t, :], y_acc[t][:], gs_t[:, t : t + 1], th[t][:], ALU.mult, ALU.mult
+            )
+
+        take_second(0)
+        take_second(1)
+        difference(0)
+        take_second(2)
+        difference(1)
+        take_second(3)
+        difference(2)
+        weigh(0)
+        difference(3)
+        weigh(1)
+        weigh(2)
+
+        old = [None] * PACK
+
+        def take_old(t, tile):
+            old[t] = tile
+            nc.vector.tensor_scalar(tile, pages[t][:].indirect(n3_l[:]), 0.5, 0.0, ALU.mult, ALU.add)
+
+        old_a = sb.tile([P, 3, S], F32, name="old_a", tag="st3")
+        take_old(0, old_a[:, 0, :])
+        weigh(3)
+        take_old(1, old_a[:, 1, :])
+        take_old(2, old_a[:, 2, :])
+
+        z_g = sb.tile([P, S, PACK], BF16, name="z_g", tag="zg", align_bytes=64)
+        for half in range(2):
+            cols = slice(half * (S // 2), (half + 1) * (S // 2))
+            nc.scalar.copy(
+                z_g[:, cols, :].rearrange("p (c i) t -> p c t i", i=4),
+                z[:, :, cols].rearrange("p t (c i) -> p c t i", i=4),
+            )
+        z_q = quantize(z_g[:].rearrange("p j t -> p (j t)"), "z")
+        old_b = sb.tile([P, S], F32, name="old_b", tag="zg", align_bytes=64)
+        take_old(3, old_b[:])
+
+        new = [None] * PACK
+
+        def larger(t):
+            acc = product((dk_words, dk_scales), z_q, t, "a")
+            new[t] = sb.tile([P, S], F32, name="new%d" % t)
+            nc.vector.scalar_tensor_tensor(new[t][:], acc[:], 0.0625, old[t], ALU.mult, ALU.max)
+
+        def put(t):
+            nc.vector.tensor_copy(pages[t][:].indirect(n3_l[:]), new[t][:])
+            nc.sync.dma_start(out.rearrange("(p t) u -> p t u", t=PACK)[:, t, :], pages[t][:])
+
+        larger(0)
+        larger(1)
+        put(0)
+        larger(2)
+        put(1)
+        larger(3)
+        put(2)
+        put(3)

@@ -1,6 +1,7 @@
 from contextlib import ExitStack
 
 import concourse.mybir as mybir
+from concourse.masks import make_identity
 
 K, T, S, H, G, U = 512, 1024, 512, 512, 2048, 1024
 FLOPS = 3 * 2 * 512 * 512 * 512
@@ -54,7 +55,7 @@ def tile_picked_twqjointbpagex_none_p_kernel(
             return raw
 
         def deal_weight(halves, name):
-            grouped = sb.tile([P, PACK, P, PACK], BF16, name=name, align_bytes=64)
+            grouped = sb.tile([P, PACK, P, PACK], BF16, name=name, tag=name, align_bytes=64)
             for half, raw in enumerate(halves):
                 nc.scalar.copy(
                     grouped[:, :, half * 64 : (half + 1) * 64, :].rearrange("p t m j -> p m j t"),
@@ -68,39 +69,49 @@ def tile_picked_twqjointbpagex_none_p_kernel(
             nc.vector.quantize_mx(out=codes[:].bitcast(FP8X4), scales=scales[:], in_=grouped)
             return codes, scales
 
-        def gather(window, lst, dtype, name):
-            picked = sb.tile([P, 512], dtype, name=name, align_bytes=64)
+        def gather(window, lst, dtype, name, tag):
+            picked = sb.tile([P, 512], dtype, name=name, tag=tag, align_bytes=64)
             nc.vector.tensor_copy(picked[:], window[:].indirect(lst[:]))
             return picked
 
-        def product(lhs, rhs, t, tag):
-            acc = psum.tile([P, S], F32, name="acc_%s%d" % (tag, t), tag="%s%d" % (tag, t))
-            cols = slice(t * P, (t + 1) * P)
+        def bank(b, name):
+            return psum.tile([P, PACK, P], F32, name=name, tag="bank%d" % b)
+
+        def flat(acc):
+            return acc[:].rearrange("p a b -> p (a b)")
+
+        def product(acc, lhs_w, lhs_s, rhs_w, rhs_s):
             nc.tensor.matmul_mx(
-                out=acc[:],
-                lhsT=lhs[0][:, cols].bitcast(FP8X4),
-                lhsT_scale=lhs[1][:, cols],
-                rhs=rhs[0][:].bitcast(FP8X4),
-                rhs_scale=rhs[1][:],
+                out=flat(acc),
+                lhsT=lhs_w.bitcast(FP8X4),
+                lhsT_scale=lhs_s,
+                rhs=rhs_w.bitcast(FP8X4),
+                rhs_scale=rhs_s,
                 start=True,
                 stop=True,
             )
-            return acc
+
+        def turn(dst, src, start, stop):
+            nc.tensor.matmul(dst, lhsT=src, rhs=ident[:], start=start, stop=stop, is_transpose=True)
+
+        def chunk(c):
+            return slice(c * P, (c + 1) * P)
 
         two_l = load_list(two, "two_l")
         offs_l = load_list(offs, "offs_l")
         xs = load_scales(x_scales, T, 0, nc.scalar, "xs")
         xw = load_words(x_words, T, "xw")
         w2_raw = [load_weight_half(w2, h, "w2_raw%d" % h) for h in range(2)]
-        dw = load_words(d_words, G, "dw")
+        w1_raw = [load_weight_half(w1, 0, "w1_raw0")]
         k1_l = load_list(k1, "k1_l")
         ds = load_scales(d_scales, G, 14, nc.sync, "ds")
+        w1_raw.append(load_weight_half(w1, 1, "w1_raw1"))
         n2_l = load_list(n2, "n2_l")
         n1_l = load_list(n1, "n1_l")
-        w1_raw = [load_weight_half(w1, h, "w1_raw%d" % h) for h in range(2)]
         gs_t = sb.tile([P, PACK], F32, name="gs_t")
         nc.sync.dma_start(gs_t[:], gs.rearrange("(p t) o -> p (t o)", t=PACK))
         n3_l = load_list(n3, "n3_l")
+        dw = load_words(d_words, G, "dw")
         pages = []
         for t in range(PACK):
             page = sb.tile([P, U], F32, name="page%d" % t)
@@ -114,111 +125,123 @@ def tile_picked_twqjointbpagex_none_p_kernel(
 
         d_win = []
         for t in range(PACK):
-            win = sb.tile([P, 2 * S], F32, name="d_win%d" % t)
+            win = sb.tile([P, 2 * S], F32, name="d_win%d" % t, tag="win%d" % t, align_bytes=64)
             nc.vector.memset(win[:, S:], 0.0)
             d_win.append(win)
         dk_scales = sb.tile([P, H], U8, name="dk_scales", align_bytes=64)
         nc.gpsimd.memset(dk_scales[:].bitcast(I32), 0)
+        ident = sb.tile([P, P], F32, name="ident")
+        make_identity(nc, ident[:])
 
-        x2_s = gather(xs, two_l, U8, "x2_s")
-        x1_s = gather(xs, offs_l, U8, "x1_s")
-        x2_w = gather(xw, two_l, U32, "x2_w")
-        x1_w = gather(xw, offs_l, U32, "x1_w")
+        x2_s = gather(xs, two_l, U8, "x2_s", "x2_s")
+        x1_s = gather(xs, offs_l, U8, "x1_s", "x1_s")
+        x2_w = gather(xw, two_l, U32, "x2_w", "x2_w")
+        x1_w = gather(xw, offs_l, U32, "x1_w", "x1_w")
 
         w2_g = deal_weight(w2_raw, "w2_g")
         w2_q = quantize(w2_g[:].rearrange("p t m j -> p (t m j)"), "w2")
+        dk_s_raw = gather(ds, k1_l, U8, "dk_s_raw", "w2_g")
+        nc.sync.dma_start(dk_scales[0:100, :].bitcast(I32), dk_s_raw[14:114, :].bitcast(I32))
         for t in range(PACK):
-            acc = product(w2_q, (x2_w, x2_s), t, "a")
-            nc.scalar.copy(d_win[t][:, :S], acc[:])
-
-        dk_w_raw = gather(dw, k1_l, U32, "dk_w_raw")
-        dk_s_raw = gather(ds, k1_l, U8, "dk_s_raw")
-        dk_words = sb.tile([P, H], U32, name="dk_words", align_bytes=64)
-        nc.vector.tensor_copy(
-            dk_words[:].rearrange("p (t a b) -> p a t b", t=PACK, b=4),
-            dk_w_raw[:].rearrange("p (a b t) -> p a t b", t=PACK, b=4),
-        )
-        dk_s_dealt = sb.tile([P, H], U8, name="dk_s_dealt", align_bytes=64)
-        nc.vector.tensor_copy(
-            dk_s_dealt[:].rearrange("p (t a b) -> p a t b", t=PACK, b=16),
-            dk_s_raw[:].rearrange("p (a b t) -> p a t b", t=PACK, b=16),
-        )
-        nc.sync.dma_start(dk_scales[0:100, :].bitcast(I32), dk_s_dealt[14:114, :].bitcast(I32))
+            acc = bank(4 + t, "d_acc%d" % t)
+            product(acc, w2_q[0][:, chunk(t)], w2_q[1][:, chunk(t)], x2_w[:], x2_s[:])
+            nc.scalar.copy(d_win[t][:, :S], flat(acc))
 
         w1_g = deal_weight(w1_raw, "w1_g")
         w1_q = quantize(w1_g[:].rearrange("p t m j -> p (t m j)"), "w1")
-        y_acc = [product(w1_q, (x1_w, x1_s), t, "b") for t in range(PACK)]
+        ys = sb.tile([P, PACK, S], F32, name="ys", tag="ys")
+        for t in range(PACK):
+            acc = bank(4 + t, "y_acc%d" % t)
+            product(acc, w1_q[0][:, chunk(t)], w1_q[1][:, chunk(t)], x1_w[:], x1_s[:])
+            nc.scalar.activation(ys[:, t, :], flat(acc), ACT.Copy, scale=gs_t[:, t : t + 1])
+        ys_g = sb.tile([P, S, PACK], F32, name="ys_g")
+        for cols in (slice(0, S // 2), slice(S // 2, S)):
+            nc.scalar.copy(ys_g[:, cols, :], ys[:, :, cols].rearrange("p t j -> p j t"))
 
-        z = sb.tile([P, PACK, S], F32, name="z")
-        second = [None] * PACK
-        th = [None] * PACK
-
-        def take_second(t):
-            second[t] = sb.tile([P, S], F32, name="second%d" % t, tag="st%d" % t)
-            nc.vector.tensor_copy(second[t][:], d_win[t][:].indirect(n2_l[:]))
-
-        def difference(t):
-            diff = sb.tile([P, S], F32, name="diff%d" % t)
-            nc.vector.tensor_tensor(diff[:], d_win[t][:].indirect(n1_l[:]), second[t][:], ALU.subtract)
-            th[t] = sb.tile([P, S], F32, name="th%d" % t)
-            nc.scalar.activation(th[t][:], diff[:], ACT.Tanh, bias=bias0[:])
-
-        def weigh(t):
-            nc.vector.scalar_tensor_tensor(
-                z[:, t, :], y_acc[t][:], gs_t[:, t : t + 1], th[t][:], ALU.mult, ALU.mult
-            )
-
-        take_second(0)
-        take_second(1)
-        difference(0)
-        take_second(2)
-        difference(1)
-        take_second(3)
-        difference(2)
-        weigh(0)
-        difference(3)
-        weigh(1)
-        weigh(2)
+        diff = [bank(c, "diff%d" % c) for c in range(PACK)]
+        for t in range(PACK):
+            first = sb.tile([P, S], F32, name="first%d" % t)
+            nc.vector.tensor_copy(first[:], d_win[t][:].indirect(n1_l[:]))
+            for c in range(PACK):
+                turn(diff[c][:, t, :], first[:, chunk(c)], True, False)
+            second = sb.tile([P, S], F32, name="second%d" % t, tag="w1_g" if t == 1 else "second%d" % t, align_bytes=64)
+            nc.vector.tensor_scalar(second[:], d_win[t][:].indirect(n2_l[:]), -1.0, 0.0, ALU.mult, ALU.add)
+            for c in range(PACK):
+                turn(diff[c][:, t, :], second[:, chunk(c)], False, True)
 
         old = [None] * PACK
+        old_turned = [None] * PACK
 
         def take_old(t, tile):
             old[t] = tile
             nc.vector.tensor_scalar(tile, pages[t][:].indirect(n3_l[:]), 0.5, 0.0, ALU.mult, ALU.add)
 
-        old_a = sb.tile([P, 3, S], F32, name="old_a", tag="st3")
-        take_old(0, old_a[:, 0, :])
-        weigh(3)
-        take_old(1, old_a[:, 1, :])
-        take_old(2, old_a[:, 2, :])
+        def turn_old(t, b):
+            acc = bank(b, "old_acc%d" % t)
+            for c in range(PACK):
+                turn(acc[:, c, :], old[t][:, chunk(c)], True, True)
+            old_turned[t] = sb.tile([P, PACK, P], F32, name="old_turned%d" % t)
+            nc.scalar.mul(flat(old_turned[t]), flat(acc), -1.0)
+
+        dk_words = gather(dw, k1_l, U32, "dk_words", "win3")
+        th = sb.tile([P, PACK, S], F32, name="th", tag="ys")
+        for c in range(PACK):
+            nc.scalar.activation(th[:, c, :], flat(diff[c]), ACT.Tanh, bias=bias0[:])
+        old0 = sb.tile([P, S], F32, name="old0", tag="win2", align_bytes=64)
+        take_old(0, old0[:])
 
         z_g = sb.tile([P, S, PACK], BF16, name="z_g", tag="zg", align_bytes=64)
-        for half in range(2):
-            cols = slice(half * (S // 2), (half + 1) * (S // 2))
-            nc.scalar.copy(
-                z_g[:, cols, :].rearrange("p (c i) t -> p c t i", i=4),
-                z[:, :, cols].rearrange("p t (c i) -> p c t i", i=4),
+        z_codes = sb.tile([P, S], U32, name="z_codes", align_bytes=64)
+        z_scales = sb.tile([P, S], U8, name="z_scales", align_bytes=64)
+        h_turned = [None] * PACK
+
+        def weigh(c):
+            back = bank(4 + c, "back%d" % c)
+            for t in range(PACK):
+                turn(back[:, t, :], th[:, c, chunk(t)], True, True)
+            nc.vector.tensor_tensor(
+                z_g[:, chunk(c), :], back[:].rearrange("p t j -> p j t"), ys_g[:, chunk(c), :], ALU.mult
             )
-        z_q = quantize(z_g[:].rearrange("p j t -> p (j t)"), "z")
-        old_b = sb.tile([P, S], F32, name="old_b", tag="zg", align_bytes=64)
-        take_old(3, old_b[:])
 
-        new = [None] * PACK
+        def coded(c):
+            nc.vector.quantize_mx(
+                out=z_codes[:, chunk(c)].bitcast(FP8X4),
+                scales=z_scales[:, chunk(c)],
+                in_=z_g[:, chunk(c), :].rearrange("p j t -> p (j t)"),
+            )
+            acc = bank(4 + c, "h_acc%d" % c)
+            product(acc, z_codes[:, chunk(c)], z_scales[:, chunk(c)], dk_words[:], dk_scales[:])
+            h_turned[c] = sb.tile([P, PACK, P], F32, name="h_turned%d" % c)
+            nc.scalar.mul(h_turned[c][:], flat(acc).rearrange("p (m t) -> p t m", t=PACK), 0.0625)
 
-        def larger(t):
-            acc = product((dk_words, dk_scales), z_q, t, "a")
-            new[t] = sb.tile([P, S], F32, name="new%d" % t)
-            nc.vector.scalar_tensor_tensor(new[t][:], acc[:], 0.0625, old[t], ALU.mult, ALU.max)
+        weigh(0)
+        weigh(1)
+        coded(0)
+        weigh(2)
+        coded(1)
+        weigh(3)
+        turn_old(0, 3)
+        coded(2)
+        coded(3)
+
+        old_rest = sb.tile([P, 3, S], F32, name="old_rest", tag="zg", align_bytes=64)
 
         def put(t):
-            nc.vector.tensor_copy(pages[t][:].indirect(n3_l[:]), new[t][:])
+            gap = bank(t, "gap%d" % t)
+            for c in range(PACK):
+                turn(gap[:, c, :], old_turned[t][:, c, :], True, False)
+                turn(gap[:, c, :], h_turned[c][:, t, :], False, True)
+            rise = sb.tile([P, S], F32, name="rise%d" % t)
+            nc.scalar.activation(rise[:], flat(gap), ACT.Relu)
+            nc.vector.tensor_tensor(pages[t][:].indirect(n3_l[:]), old[t], rise[:], ALU.add)
             nc.sync.dma_start(out.rearrange("(p t) u -> p t u", t=PACK)[:, t, :], pages[t][:])
 
-        larger(0)
-        larger(1)
+        for t in range(1, PACK):
+            take_old(t, old_rest[:, t - 1, :])
         put(0)
-        larger(2)
+        turn_old(1, 7)
         put(1)
-        larger(3)
+        turn_old(2, 0)
         put(2)
+        turn_old(3, 1)
         put(3)

from contextlib import ExitStack

import concourse.mybir as mybir
from concourse.masks import make_identity

K, T, S, H, G, U = 512, 1024, 512, 512, 2048, 1024
FLOPS = 3 * 2 * 512 * 512 * 512

F32 = mybir.dt.float32
BF16 = mybir.dt.bfloat16
I32 = mybir.dt.int32
U32 = mybir.dt.uint32
U16 = mybir.dt.uint16
U8 = mybir.dt.uint8
FP8X4 = mybir.dt.float8_e4m3fn_x4
ALU = mybir.AluOpType
ACT = mybir.ActivationFunctionType

P = 128
PACK = 4


def tile_picked_twqjointbpagex_none_p_kernel(
    tc, x_words, x_scales, w1, w2, gs, d_words, d_scales, mem, offs, two, n1, n2, k1, n3, out
):
    nc = tc.nc
    with ExitStack() as ctx:
        sb = ctx.enter_context(tc.tile_pool(name="sb", bufs=1))
        psum = ctx.enter_context(tc.psum_pool(name="psum", bufs=1))

        def load_list(src, name):
            tile = sb.tile([P, S // 16], U16, name=name)
            nc.sync.dma_start(tile[:], src)
            return tile

        def load_words(src, width, name):
            tile = sb.tile([P, width], U32, name=name)
            nc.sync.dma_start(tile[:].bitcast(I32), src[0].rearrange("p c r -> p (c r)").bitcast(I32))
            return tile

        def load_scales(src, width, first, queue, name):
            tile = sb.tile([P, width], U8, name=name)
            nc.gpsimd.memset(tile[:].bitcast(I32), 0)
            for q in range(4):
                queue.dma_start(
                    tile[32 * q + first : 32 * q + first + 4, :].bitcast(I32),
                    src[0, 4 * q : 4 * q + 4, :].bitcast(I32),
                )
            return tile

        def load_weight_half(w, half, name):
            raw = sb.tile([P, PACK, H // 2], F32, name=name)
            cols = slice(half * (H // 2), (half + 1) * (H // 2))
            nc.sync.dma_start(raw[:], w.rearrange("(p j) c -> p j c", j=PACK)[:, :, cols])
            return raw

        def deal_weight(halves, name):
            grouped = sb.tile([P, PACK, P, PACK], BF16, name=name, tag=name, align_bytes=64)
            for half, raw in enumerate(halves):
                nc.scalar.copy(
                    grouped[:, :, half * 64 : (half + 1) * 64, :].rearrange("p t m j -> p m j t"),
                    raw[:].rearrange("p j (m t) -> p m j t", t=PACK),
                )
            return grouped

        def quantize(grouped, name):
            codes = sb.tile([P, 512], U32, name=name + "_codes", align_bytes=64)
            scales = sb.tile([P, 512], U8, name=name + "_scales", align_bytes=64)
            nc.vector.quantize_mx(out=codes[:].bitcast(FP8X4), scales=scales[:], in_=grouped)
            return codes, scales

        def gather(window, lst, dtype, name, tag):
            picked = sb.tile([P, 512], dtype, name=name, tag=tag, align_bytes=64)
            nc.vector.tensor_copy(picked[:], window[:].indirect(lst[:]))
            return picked

        def bank(b, name):
            return psum.tile([P, PACK, P], F32, name=name, tag="bank%d" % b)

        def flat(acc):
            return acc[:].rearrange("p a b -> p (a b)")

        def product(acc, lhs_w, lhs_s, rhs_w, rhs_s):
            nc.tensor.matmul_mx(
                out=flat(acc),
                lhsT=lhs_w.bitcast(FP8X4),
                lhsT_scale=lhs_s,
                rhs=rhs_w.bitcast(FP8X4),
                rhs_scale=rhs_s,
                start=True,
                stop=True,
            )

        def turn(dst, src, start, stop):
            nc.tensor.matmul(dst, lhsT=src, rhs=ident[:], start=start, stop=stop, is_transpose=True)

        def chunk(c):
            return slice(c * P, (c + 1) * P)

        two_l = load_list(two, "two_l")
        offs_l = load_list(offs, "offs_l")
        xs = load_scales(x_scales, T, 0, nc.scalar, "xs")
        xw = load_words(x_words, T, "xw")
        w2_raw = [load_weight_half(w2, h, "w2_raw%d" % h) for h in range(2)]
        w1_raw = [load_weight_half(w1, 0, "w1_raw0")]
        k1_l = load_list(k1, "k1_l")
        ds = load_scales(d_scales, G, 14, nc.sync, "ds")
        w1_raw.append(load_weight_half(w1, 1, "w1_raw1"))
        n2_l = load_list(n2, "n2_l")
        n1_l = load_list(n1, "n1_l")
        gs_t = sb.tile([P, PACK], F32, name="gs_t")
        nc.sync.dma_start(gs_t[:], gs.rearrange("(p t) o -> p (t o)", t=PACK))
        n3_l = load_list(n3, "n3_l")
        dw = load_words(d_words, G, "dw")
        pages = []
        for t in range(PACK):
            page = sb.tile([P, U], F32, name="page%d" % t)
            nc.sync.dma_start(page[:], mem.rearrange("(p t) u -> p t u", t=PACK)[:, t, :])
            pages.append(page)

        zero = sb.tile([P, 1], F32, name="zero")
        nc.gpsimd.memset(zero[:], 0.0)
        bias0 = sb.tile([P, 1], F32, name="bias0")
        nc.scalar.activation(bias0[:], zero[:], ACT.Tanh)

        d_win = []
        for t in range(PACK):
            win = sb.tile([P, 2 * S], F32, name="d_win%d" % t, tag="win%d" % t, align_bytes=64)
            nc.vector.memset(win[:, S:], 0.0)
            d_win.append(win)
        dk_scales = sb.tile([P, H], U8, name="dk_scales", align_bytes=64)
        nc.gpsimd.memset(dk_scales[:].bitcast(I32), 0)
        ident = sb.tile([P, P], F32, name="ident")
        make_identity(nc, ident[:])

        x2_s = gather(xs, two_l, U8, "x2_s", "x2_s")
        x1_s = gather(xs, offs_l, U8, "x1_s", "x1_s")
        x2_w = gather(xw, two_l, U32, "x2_w", "x2_w")
        x1_w = gather(xw, offs_l, U32, "x1_w", "x1_w")

        w2_g = deal_weight(w2_raw, "w2_g")
        w2_q = quantize(w2_g[:].rearrange("p t m j -> p (t m j)"), "w2")
        dk_s_raw = gather(ds, k1_l, U8, "dk_s_raw", "w2_g")
        nc.sync.dma_start(dk_scales[0:100, :].bitcast(I32), dk_s_raw[14:114, :].bitcast(I32))
        for t in range(PACK):
            acc = bank(4 + t, "d_acc%d" % t)
            product(acc, w2_q[0][:, chunk(t)], w2_q[1][:, chunk(t)], x2_w[:], x2_s[:])
            nc.scalar.copy(d_win[t][:, :S], flat(acc))

        w1_g = deal_weight(w1_raw, "w1_g")
        w1_q = quantize(w1_g[:].rearrange("p t m j -> p (t m j)"), "w1")
        ys = sb.tile([P, PACK, S], F32, name="ys", tag="ys")
        for t in range(PACK):
            acc = bank(4 + t, "y_acc%d" % t)
            product(acc, w1_q[0][:, chunk(t)], w1_q[1][:, chunk(t)], x1_w[:], x1_s[:])
            nc.scalar.activation(ys[:, t, :], flat(acc), ACT.Copy, scale=gs_t[:, t : t + 1])
        ys_g = sb.tile([P, S, PACK], F32, name="ys_g")
        for cols in (slice(0, S // 2), slice(S // 2, S)):
            nc.scalar.copy(ys_g[:, cols, :], ys[:, :, cols].rearrange("p t j -> p j t"))

        diff = [bank(c, "diff%d" % c) for c in range(PACK)]
        for t in range(PACK):
            first = sb.tile([P, S], F32, name="first%d" % t)
            nc.vector.tensor_copy(first[:], d_win[t][:].indirect(n1_l[:]))
            for c in range(PACK):
                turn(diff[c][:, t, :], first[:, chunk(c)], True, False)
            second = sb.tile([P, S], F32, name="second%d" % t, tag="w1_g" if t == 1 else "second%d" % t, align_bytes=64)
            nc.vector.tensor_scalar(second[:], d_win[t][:].indirect(n2_l[:]), -1.0, 0.0, ALU.mult, ALU.add)
            for c in range(PACK):
                turn(diff[c][:, t, :], second[:, chunk(c)], False, True)

        old = [None] * PACK
        old_turned = [None] * PACK

        def take_old(t, tile):
            old[t] = tile
            nc.vector.tensor_scalar(tile, pages[t][:].indirect(n3_l[:]), 0.5, 0.0, ALU.mult, ALU.add)

        def turn_old(t, b):
            acc = bank(b, "old_acc%d" % t)
            for c in range(PACK):
                turn(acc[:, c, :], old[t][:, chunk(c)], True, True)
            old_turned[t] = sb.tile([P, PACK, P], F32, name="old_turned%d" % t)
            nc.scalar.mul(flat(old_turned[t]), flat(acc), -1.0)

        dk_words = gather(dw, k1_l, U32, "dk_words", "win3")
        th = sb.tile([P, PACK, S], F32, name="th", tag="ys")
        for c in range(PACK):
            nc.scalar.activation(th[:, c, :], flat(diff[c]), ACT.Tanh, bias=bias0[:])
        old0 = sb.tile([P, S], F32, name="old0", tag="win2", align_bytes=64)
        take_old(0, old0[:])

        z_g = sb.tile([P, S, PACK], BF16, name="z_g", tag="zg", align_bytes=64)
        z_codes = sb.tile([P, S], U32, name="z_codes", align_bytes=64)
        z_scales = sb.tile([P, S], U8, name="z_scales", align_bytes=64)
        h_turned = [None] * PACK

        def weigh(c):
            back = bank(4 + c, "back%d" % c)
            for t in range(PACK):
                turn(back[:, t, :], th[:, c, chunk(t)], True, True)
            nc.vector.tensor_tensor(
                z_g[:, chunk(c), :], back[:].rearrange("p t j -> p j t"), ys_g[:, chunk(c), :], ALU.mult
            )

        def coded(c):
            nc.vector.quantize_mx(
                out=z_codes[:, chunk(c)].bitcast(FP8X4),
                scales=z_scales[:, chunk(c)],
                in_=z_g[:, chunk(c), :].rearrange("p j t -> p (j t)"),
            )
            acc = bank(4 + c, "h_acc%d" % c)
            product(acc, z_codes[:, chunk(c)], z_scales[:, chunk(c)], dk_words[:], dk_scales[:])
            h_turned[c] = sb.tile([P, PACK, P], F32, name="h_turned%d" % c)
            nc.scalar.mul(h_turned[c][:], flat(acc).rearrange("p (m t) -> p t m", t=PACK), 0.0625)

        weigh(0)
        weigh(1)
        coded(0)
        weigh(2)
        coded(1)
        weigh(3)
        turn_old(0, 3)
        coded(2)
        coded(3)

        old_rest = sb.tile([P, 3, S], F32, name="old_rest", tag="zg", align_bytes=64)

        def put(t):
            gap = bank(t, "gap%d" % t)
            for c in range(PACK):
                turn(gap[:, c, :], old_turned[t][:, c, :], True, False)
                turn(gap[:, c, :], h_turned[c][:, t, :], False, True)
            rise = sb.tile([P, S], F32, name="rise%d" % t)
            nc.scalar.activation(rise[:], flat(gap), ACT.Relu)
            nc.vector.tensor_tensor(pages[t][:].indirect(n3_l[:]), old[t], rise[:], ALU.add)
            nc.sync.dma_start(out.rearrange("(p t) u -> p t u", t=PACK)[:, t, :], pages[t][:])

        for t in range(1, PACK):
            take_old(t, old_rest[:, t - 1, :])
        put(0)
        turn_old(1, 7)
        put(1)
        turn_old(2, 0)
        put(2)
        turn_old(3, 1)
        put(3)
